import numpy as np
import ml_dtypes


def mxq(x, axis, fmt="e4m3"):
    dtype, down = {"e4m3": (ml_dtypes.float8_e4m3fn, 7), "e5m2": (ml_dtypes.float8_e5m2, 14)}[fmt]
    v = np.moveaxis(np.asarray(x, np.float32).astype(ml_dtypes.bfloat16).astype(np.float64), axis, -1)
    blocks = v.reshape(v.shape[:-1] + (-1, 32))
    amax = np.abs(blocks).max(-1, keepdims=True)
    byte = np.maximum(np.where(amax > 0, np.frexp(amax)[1] - 1 + 127, 0) - down, 1)
    scale = np.exp2(byte - 127.0)
    codes = (blocks / scale).astype(np.float32).astype(dtype).astype(np.float64)
    return np.moveaxis((codes * scale).reshape(v.shape), -1, axis)


WIDE = False


def mx_kscale(k):
    if not WIDE:
        return np.ones(k)
    levels = np.array([10, -10, 5, -5, 0])
    if k % 512:
        return np.exp2(np.random.permutation(np.resize(levels, k // 32))).repeat(32)
    a = np.empty((k // 512, 16))
    for p in range(k // 512):
        a[p, :8] = np.random.permutation(np.resize(levels, 8))
        for g in range(8):
            far = levels[np.abs(levels - a[p, g]) >= 10]
            a[p, g + 8] = far[np.random.randint(len(far))]
    return np.exp2(a.ravel()).repeat(32)


def f64(x):
    return np.asarray(x).astype(np.float64)


def striped(idx):
    return np.tile(idx.reshape(-1, 16).T, (8, 1)).astype(np.uint16)


def unstriped(offs):
    return offs[:16].T.reshape(-1).astype(np.int64)


E2M1 = np.array([0.0, 0.5, 1.0, 1.5, 2.0, 3.0, 4.0, 6.0, -0.0, -0.5, -1.0, -1.5, -2.0, -3.0, -4.0, -6.0])


def pack_weight(w, fmt):
    k, n = w.shape
    w = f64(np.asarray(w, np.float32).astype(ml_dtypes.bfloat16)).reshape(k // 32, 32, n)
    amax = np.abs(w).max(1)
    if fmt == "e4m3":
        byte = np.frexp(amax)[1] - 1 + 127 - 7
    else:
        mant, ex = np.frexp(amax / 6.0)
        byte = np.where(mant > 0.5, ex, ex - 1) + 127
    byte = np.clip(np.where(amax > 0, byte, 1), 1, 254)
    scaled = (w * np.exp2(127.0 - byte)[:, None, :]).reshape(k, n).astype(np.float32)
    by_word = np.ascontiguousarray(scaled.reshape(k // 512, 128, 4, n).transpose(0, 1, 3, 2))
    if fmt == "e4m3":
        words = by_word.astype(ml_dtypes.float8_e4m3fn).view(np.uint8)
    else:
        c = by_word.astype(ml_dtypes.float4_e2m1fn).view(np.uint8) & 0xF
        words = (c[..., 0::2] | (c[..., 1::2] << 4)).reshape(k // 512, 128, 2 * n)
    return np.ascontiguousarray(words), np.ascontiguousarray(byte.astype(np.uint8).reshape(k // 512, 16, n))


def unpack_weight(words, scales, fmt):
    g, _, n = scales.shape
    words = np.ascontiguousarray(words).reshape(g, 128, n, -1)
    if fmt == "e4m3":
        vals = words.view(ml_dtypes.float8_e4m3fn).astype(np.float64)
    else:
        nib = np.empty((g, 128, n, 4), np.uint8)
        nib[..., 0::2] = words & 0xF
        nib[..., 1::2] = words >> 4
        vals = E2M1[nib]
    vals = vals * np.repeat(np.exp2(scales.astype(np.float64) - 127.0), 8, axis=1)[..., None]
    return vals.transpose(0, 1, 3, 2).reshape(g * 512, n)


def gelu(v):
    return 0.5 * v * (1.0 + np.tanh(np.sqrt(2.0 / np.pi) * (v + 0.044715 * v**3)))


K, T, S, H, T3, S2, T2 = 1024, 2048, 1024, 512, 2048, 512, 2048

def setup_inputs():
    n = np.random.standard_normal
    s = mx_kscale(K)[:, None]
    u = mx_kscale(H)[:, None]
    tab_words, tab_scales = pack_weight(n((K, T)) * s, "e4m3")
    w4_words, w4_scales = pack_weight(1.8 * n((K, H)) / np.sqrt(K) / s * u.T, "e2m1")
    tab2_words, tab2_scales = pack_weight(n((H, T3)) / np.sqrt(H) / u, "e4m3")
    return {
        "tab_words": tab_words, "tab_scales": tab_scales,
        "offs": striped(np.random.permutation(T)[:S]),
        "w1": (1.8 * n((K, H)) / np.sqrt(K) / s * u.T).astype(np.float32),
        "w2": (1.8 * n((K, H)) / np.sqrt(K) / s * u.T).astype(np.float32),
        "w4_words": w4_words, "w4_scales": w4_scales,
        "tab2_words": tab2_words, "tab2_scales": tab2_scales,
        "offs2": striped(np.random.permutation(T3)[:S2]),
        "grade_gain": np.exp(0.3 * n(S2)).astype(np.float32),
        "grade_shift": (0.5 * n(S2)).astype(np.float32),
        "offs3": striped(np.random.permutation(T2)[:S]),
        "wgo": np.exp(0.3 * n((128, S))).astype(np.float32),
        "page1": n((S2, T2)).astype(np.float32),
    }

def reference(tab_words, tab_scales, offs, w1, w2, w4_words, w4_scales, tab2_words, tab2_scales, offs2,
              grade_gain, grade_shift, offs3, wgo, page1):
    v = unpack_weight(tab_words, tab_scales, "e4m3")[:, unstriped(offs)]
    v2 = unpack_weight(tab2_words, tab2_scales, "e4m3")[:, unstriped(offs2)]
    w4 = unpack_weight(w4_words, w4_scales, "e2m1")
    skill1 = mxq(f64(w1), 0, "e4m3").T @ v
    skill2 = mxq(f64(w2), 0, "e4m3").T @ v
    spirit = w4.T @ v
    h = np.minimum(np.maximum(skill1, skill2), spirit)
    hq = mxq(h, 0, "e4m3")
    e = v2.T @ hq
    y = np.tanh(e) * f64(grade_gain)[:, None] + f64(grade_shift)[:, None]
    out = f64(page1).copy()
    out[:, unstriped(offs3)] = np.tile(f64(wgo), (S2 // 128, 1)) * y
    return out

@@ -1,0 +1,255 @@
+from contextlib import ExitStack
+
+import concourse.mybir as mybir
+
+K, T, S, H, T3, S2, T2 = 1024, 2048, 1024, 512, 2048, 512, 2048
+FLOPS = 2 * (3 * K * H * S + H * S2 * S)
+
+F32 = mybir.dt.float32
+BF16 = mybir.dt.bfloat16
+I32 = mybir.dt.int32
+U32 = mybir.dt.uint32
+U16 = mybir.dt.uint16
+U8 = mybir.dt.uint8
+FP8X4 = mybir.dt.float8_e4m3fn_x4
+FP4X4 = mybir.dt.float4_e2m1fn_x4
+ACT = mybir.ActivationFunctionType
+ALU = mybir.AluOpType
+
+P = 128
+PACK = 4
+PASSES = K // (P * PACK)
+CHUNK = 128
+CHUNKS = S // CHUNK
+HALF = 512
+M_TILES = S2 // P
+
+
+def tile_list_kendo_panel_scores_kernel(
+    tc, tab_words, tab_scales, offs, w1, w2, w4_words, w4_scales, tab2_words, tab2_scales, offs2,
+    grade_gain, grade_shift, offs3, wgo, page1, out,
+):
+    nc = tc.nc
+    with ExitStack() as ctx:
+        keep = ctx.enter_context(tc.tile_pool(name="keep", bufs=1))
+        ring = ctx.enter_context(tc.tile_pool(name="ring", bufs=2))
+        psum = ctx.enter_context(tc.psum_pool(name="psum", bufs=1))
+
+        def tile(shape, dtype, name, tag=None):
+            return keep.tile(shape, dtype, name=name, tag=tag or name, align_bytes=64)
+
+        idx = tile([P, S // 16], U16, "idx")
+        idx2 = tile([P, S2 // 16], U16, "idx2")
+        idx3 = tile([P, S // 16], U16, "idx3")
+
+        tab_w = [tile([P, T], U32, "tab_w%d" % a) for a in range(PASSES)]
+        tab_s = tile([P, T], U8, "tab_s")
+        tab2_w = tile([P, T3], U32, "tab2_w")
+        tab2_s = tile([P, T3], U8, "tab2_s")
+        w4_raw = tile([P, PASSES, H], U16, "w4_raw")
+        w4s_raw = tile([P, PASSES, H], U8, "w4s_raw")
+
+        nc.vector.memset(tab_s[:].bitcast(I32), 0)
+        nc.vector.memset(w4s_raw[:].bitcast(I32), 0)
+        nc.vector.memset(tab2_s[:].bitcast(I32), 0)
+        v_s_low = tile([P, S], U8, "v_s_low")
+        nc.vector.memset(v_s_low[:].bitcast(I32), 0)
+
+        def load_scale_rows(dst, src):
+            rows = src.rearrange("a (q r) n -> r q a n", r=4)
+            for r in range(4):
+                nc.sync.dma_start(out=dst[r:P:32].bitcast(I32), in_=rows[r].bitcast(I32))
+
+        def load_words(dst, src):
+            nc.sync.dma_start(out=dst[:].bitcast(I32), in_=src.rearrange("p t i -> p (t i)").bitcast(I32))
+
+        def load_weight(w, a, cols, name):
+            raw = tile([P, PACK, cols.stop - cols.start], F32, name)
+            rows = w[a * 512 : (a + 1) * 512, cols].rearrange("(p j) c -> p j c", j=PACK)
+            nc.sync.dma_start(out=raw[:], in_=rows)
+            return raw
+
+        whole, low, high = slice(0, H), slice(0, H // 2), slice(H // 2, H)
+        nc.sync.dma_start(idx[:], offs)
+        nc.sync.dma_start(out=w4_raw[:].bitcast(I32), in_=w4_words.rearrange("a p n -> p a n").bitcast(I32))
+        for q in range(4):
+            nc.sync.dma_start(
+                out=tab_s[32 * q : 32 * q + 8, :].bitcast(I32), in_=tab_scales[:, 4 * q : 4 * q + 4, :].bitcast(I32)
+            )
+        load_words(tab_w[0], tab_words[0])
+        w1_raw0 = load_weight(w1, 0, whole, "w1_raw0")
+        load_scale_rows(w4s_raw, w4_scales)
+        w1_raw1 = load_weight(w1, 1, whole, "w1_raw1")
+        nc.sync.dma_start(idx2[:], offs2)
+        load_scale_rows(tab2_s[:].rearrange("p (a n) -> p a n", a=1), tab2_scales)
+        load_words(tab_w[1], tab_words[1])
+        w2_raw0 = load_weight(w2, 0, whole, "w2_raw0")
+        w2_raw1l = load_weight(w2, 1, low, "w2_raw1l")
+        w2_raw1h = load_weight(w2, 1, high, "w2_raw1h")
+        load_words(tab2_w, tab2_words[0])
+        nc.sync.dma_start(idx3[:], offs3)
+        gain = tile([P, M_TILES], F32, "gain")
+        shift = tile([P, M_TILES], F32, "shift")
+        with nc.allow_non_contiguous_dma(reason="one value a partition"):
+            nc.sync.dma_start(out=gain[:], in_=grade_gain.rearrange("(c p) -> p c", p=P))
+            nc.sync.dma_start(out=shift[:], in_=grade_shift.rearrange("(c p) -> p c", p=P))
+        wgo_sb = tile([P, S], F32, "wgo_sb")
+        nc.sync.dma_start(out=wgo_sb[:], in_=wgo)
+        pages = [tile([P, T2], F32, "page%d" % m) for m in range(M_TILES)]
+        for m in range(M_TILES):
+            nc.sync.dma_start(out=pages[m][:], in_=page1[m * P : (m + 1) * P, :])
+
+        v_w = [tile([P, S], U32, "v_w%d" % a) for a in range(PASSES)]
+        v_s = tile([P, S], U8, "v_s")
+        v2_w = tile([P, S2], U32, "v2_w")
+        v2_s = tile([P, S2], U8, "v2_s")
+
+        def gather(dst, window, offsets, j0, j1):
+            nc.vector.tensor_copy(dst[:, j0:j1], window.indirect(offsets[:, j0 // 16 : j1 // 16]))
+
+        rounded = {}
+        codes = {}
+        planes = {}
+
+        def round_weight(copy, key, raw, cols):
+            if key not in rounded:
+                rounded[key] = tile([P, PACK * H], BF16, "rounded_%s%d" % key)
+            m_range = slice(cols.start // 4, cols.stop // 4)
+            dst = rounded[key][:].rearrange("p (t m j) -> p m j t", t=4, j=PACK)[:, m_range]
+            copy(out=dst, in_=raw[:].rearrange("p j (m t) -> p m j t", t=4))
+
+        def quantize_weight(key):
+            codes[key] = tile([P, H], U32, "codes_%s%d" % key)
+            planes[key] = tile([P, H], U8, "plane_%s%d" % key)
+            nc.vector.quantize_mx(out=codes[key][:].bitcast(FP8X4), scales=planes[key][:], in_=rounded[key][:])
+
+        w4_c = tile([P, PASSES, H], U16, "w4_c")
+        nc.vector.tensor_copy(
+            out=w4_c[:].rearrange("p a (t m) -> p a t m", t=4), in_=w4_raw[:].rearrange("p a (m t) -> p a t m", t=4)
+        )
+        gather(v_s, tab_s[:], idx, 0, S)
+        for q in range(4):
+            nc.gpsimd.dma_start(
+                out=v_s_low[32 * q : 32 * q + 4, :].bitcast(I32), in_=v_s[32 * q + 4 : 32 * q + 8, :].bitcast(I32)
+            )
+        gather(v_w[0], tab_w[0][:], idx, 0, S)
+        round_weight(nc.scalar.copy, ("w1", 0), w1_raw0, whole)
+        round_weight(nc.scalar.copy, ("w1", 1), w1_raw1, whole)
+        round_weight(nc.scalar.copy, ("w2", 0), w2_raw0, whole)
+        w4_s = tile([P, PASSES, H], U8, "w4_s")
+        nc.vector.tensor_copy(
+            out=w4_s[:].rearrange("p a (t m) -> p a t m", t=4), in_=w4s_raw[:].rearrange("p a (m t) -> p a t m", t=4)
+        )
+        quantize_weight(("w1", 0))
+        gather(v2_s, tab2_s[:], idx2, 0, S2)
+        quantize_weight(("w1", 1))
+        gather(v_w[1], tab_w[1][:], idx, 0, 256)
+        gather(v_w[1], tab_w[1][:], idx, 256, S)
+        quantize_weight(("w2", 0))
+        round_weight(nc.vector.tensor_copy, ("w2", 1), w2_raw1l, low)
+        round_weight(nc.vector.tensor_copy, ("w2", 1), w2_raw1h, high)
+        quantize_weight(("w2", 1))
+
+        def product(bank, c, weight):
+            cols = slice(c * CHUNK, (c + 1) * CHUNK)
+            for t in range(4):
+                stat = slice(t * P, (t + 1) * P)
+                for a in range(PASSES):
+                    if weight == "w4":
+                        lhsT, lhsT_scale = w4_c[:, a, stat].bitcast(FP4X4), w4_s[:, a, stat]
+                        rhs_scale = (v_s, v_s_low)[a][:, cols]
+                    else:
+                        lhsT, lhsT_scale = codes[(weight, a)][:, stat].bitcast(FP8X4), planes[(weight, a)][:, stat]
+                        rhs_scale = v_s[4 * a : P, cols]
+                    nc.tensor.matmul_mx(
+                        out=bank[:, t, :], lhsT=lhsT, lhsT_scale=lhsT_scale,
+                        rhs=v_w[a][:, cols].bitcast(FP8X4), rhs_scale=rhs_scale,
+                        start=(a == 0), stop=(a == PASSES - 1),
+                    )
+            return bank[:].rearrange("p t n -> p n t")
+
+        early = tile([P, CHUNKS // 2, CHUNK, PACK], F32, "skill1_early", tag="w2_raw0")
+        late = tile([P, CHUNKS // 2, CHUNK, PACK], F32, "skill1_late")
+        skill1 = [part[:, c] for part in (early, late) for c in range(CHUNKS // 2)]
+        best = {}
+        spirit = {}
+        h_bf = [tile([P, HALF, PACK], BF16, "h_bf%d" % u) for u in range(2)]
+        h_c = [tile([P, HALF], U32, "h_c%d" % u) for u in range(2)]
+        h_s = [tile([P, HALF], U8, "h_s%d" % u) for u in range(2)]
+
+        def first_reading(c):
+            bank = psum.tile([P, 4, CHUNK], F32, name="bank_a", tag="bank_a", bufs=3)
+            sums = product(bank, c, "w1")
+            nc.scalar.copy(out=skill1[c], in_=sums)
+
+        def better_reading(c):
+            bank4 = psum.tile([P, 4, CHUNK], F32, name="bank_sp", tag="bank_sp", bufs=3)
+            spirit[c] = product(bank4, c, "w4")
+            bank2 = psum.tile([P, 4, CHUNK], F32, name="bank_s2", tag="bank_s2", bufs=2)
+            sums = product(bank2, c, "w2")
+            best[c] = ring.tile([P, CHUNK, PACK], F32, name="best", tag="pair", bufs=2)
+            nc.vector.tensor_tensor(out=best[c][:], in0=sums, in1=skill1[c], op=ALU.max)
+
+        def cap(c):
+            u, n0 = divmod(c * CHUNK, HALF)
+            nc.vector.tensor_tensor(out=h_bf[u][:, n0 : n0 + CHUNK, :], in0=spirit[c], in1=best[c][:], op=ALU.min)
+
+        def quantize_h(u):
+            nc.vector.quantize_mx(
+                out=h_c[u][:].bitcast(FP8X4), scales=h_s[u][:], in_=h_bf[u][:].rearrange("p n t -> p (n t)")
+            )
+
+        scores = {}
+
+        def score(m, u):
+            rows = slice(m * P, (m + 1) * P)
+            bank = psum.tile([P, HALF], F32, name="bank_a", tag="bank_a", bufs=3)
+            nc.tensor.matmul_mx(
+                out=bank[:], lhsT=v2_w[:, rows].bitcast(FP8X4), lhsT_scale=v2_s[:, rows],
+                rhs=h_c[u][:].bitcast(FP8X4), rhs_scale=h_s[u][:], start=True, stop=True,
+            )
+            bent = ring.tile([P, HALF], F32, name="bent", tag="bent", bufs=2)
+            nc.scalar.activation(out=bent[:], in_=bank[:], func=ACT.Tanh)
+            scores[(m, u)] = ring.tile([P, HALF], F32, name="scores", tag="pair", bufs=2)
+            nc.scalar.activation(
+                out=scores[(m, u)][:], in_=bent[:], func=ACT.Identity,
+                scale=gain[:, m : m + 1], bias=shift[:, m : m + 1],
+            )
+
+        def put(m, u):
+            j0, j1 = u * HALF, (u + 1) * HALF
+            nc.vector.tensor_tensor(
+                out=pages[m][:].indirect(idx3[:, j0 // 16 : j1 // 16]),
+                in0=scores[(m, u)][:], in1=wgo_sb[:, j0:j1], op=ALU.mult,
+            )
+
+        def store(m):
+            nc.sync.dma_start(out=out[m * P : (m + 1) * P, :], in_=pages[m][:])
+
+        def finish(m, u):
+            score(m, u)
+            put(m, u)
+            if u == 1:
+                store(m)
+
+        ahead = 3
+        for c in range(ahead):
+            first_reading(c)
+        for c in range(CHUNKS):
+            better_reading(c)
+            if c + ahead < CHUNKS:
+                first_reading(c + ahead)
+            if c > 0:
+                cap(c - 1)
+            if c == 2:
+                gather(v2_w, tab2_w[:], idx2, 0, S2)
+            if c == CHUNKS // 2:
+                quantize_h(0)
+            if c in (5, 6):
+                finish(c - 5, 0)
+        cap(CHUNKS - 1)
+        quantize_h(1)
+        for m in range(2, M_TILES):
+            finish(m, 0)
+        for m in range(M_TILES):
+            finish(m, 1)

@@ -55,10 +55,10 @@ def tile_list_kendo_panel_scores_kernel(
         v_s_low = tile([P, S], U8, "v_s_low")
         nc.vector.memset(v_s_low[:].bitcast(I32), 0)
 
-        def load_scale_rows(dst, src):
+        def load_scale_rows(dst, src, first=0):
             rows = src.rearrange("a (q r) n -> r q a n", r=4)
             for r in range(4):
-                nc.sync.dma_start(out=dst[r:P:32].bitcast(I32), in_=rows[r].bitcast(I32))
+                nc.sync.dma_start(out=dst[first + r : P : 32].bitcast(I32), in_=rows[r].bitcast(I32))
 
         def load_words(dst, src):
             nc.sync.dma_start(out=dst[:].bitcast(I32), in_=src.rearrange("p t i -> p (t i)").bitcast(I32))
@@ -81,7 +81,7 @@ def tile_list_kendo_panel_scores_kernel(
         load_scale_rows(w4s_raw, w4_scales)
         w1_raw1 = load_weight(w1, 1, whole, "w1_raw1")
         nc.sync.dma_start(idx2[:], offs2)
-        load_scale_rows(tab2_s[:].rearrange("p (a n) -> p a n", a=1), tab2_scales)
+        load_scale_rows(tab2_s[:].rearrange("p (a n) -> p a n", a=1), tab2_scales, first=8)
         load_words(tab_w[1], tab_words[1])
         w2_raw0 = load_weight(w2, 0, whole, "w2_raw0")
         w2_raw1l = load_weight(w2, 1, low, "w2_raw1l")
@@ -128,10 +128,7 @@ def tile_list_kendo_panel_scores_kernel(
             out=w4_c[:].rearrange("p a (t m) -> p a t m", t=4), in_=w4_raw[:].rearrange("p a (m t) -> p a t m", t=4)
         )
         gather(v_s, tab_s[:], idx, 0, S)
-        for q in range(4):
-            nc.gpsimd.dma_start(
-                out=v_s_low[32 * q : 32 * q + 4, :].bitcast(I32), in_=v_s[32 * q + 4 : 32 * q + 8, :].bitcast(I32)
-            )
+        nc.gpsimd.dma_start(out=v_s_low[0:100, :].bitcast(I32), in_=v_s[4:104, :].bitcast(I32))
         gather(v_w[0], tab_w[0][:], idx, 0, S)
         round_weight(nc.scalar.copy, ("w1", 0), w1_raw0, whole)
         round_weight(nc.scalar.copy, ("w1", 1), w1_raw1, whole)
@@ -145,27 +142,27 @@ def tile_list_kendo_panel_scores_kernel(
         quantize_weight(("w1", 1))
         gather(v_w[1], tab_w[1][:], idx, 0, 256)
         gather(v_w[1], tab_w[1][:], idx, 256, S)
-        quantize_weight(("w2", 0))
         round_weight(nc.vector.tensor_copy, ("w2", 1), w2_raw1l, low)
+        quantize_weight(("w2", 0))
         round_weight(nc.vector.tensor_copy, ("w2", 1), w2_raw1h, high)
         quantize_weight(("w2", 1))
 
         def product(bank, c, weight):
             cols = slice(c * CHUNK, (c + 1) * CHUNK)
-            for t in range(4):
+            steps = [(a, t) for a in range(PASSES) for t in range(4)]
+            for a, t in steps:
                 stat = slice(t * P, (t + 1) * P)
-                for a in range(PASSES):
-                    if weight == "w4":
-                        lhsT, lhsT_scale = w4_c[:, a, stat].bitcast(FP4X4), w4_s[:, a, stat]
-                        rhs_scale = (v_s, v_s_low)[a][:, cols]
-                    else:
-                        lhsT, lhsT_scale = codes[(weight, a)][:, stat].bitcast(FP8X4), planes[(weight, a)][:, stat]
-                        rhs_scale = v_s[4 * a : P, cols]
-                    nc.tensor.matmul_mx(
-                        out=bank[:, t, :], lhsT=lhsT, lhsT_scale=lhsT_scale,
-                        rhs=v_w[a][:, cols].bitcast(FP8X4), rhs_scale=rhs_scale,
-                        start=(a == 0), stop=(a == PASSES - 1),
-                    )
+                if weight == "w4":
+                    lhsT, lhsT_scale = w4_c[:, a, stat].bitcast(FP4X4), w4_s[:, a, stat]
+                    rhs_scale = (v_s, v_s_low)[a][:, cols]
+                else:
+                    lhsT, lhsT_scale = codes[(weight, a)][:, stat].bitcast(FP8X4), planes[(weight, a)][:, stat]
+                    rhs_scale = v_s[4 * a : P, cols]
+                nc.tensor.matmul_mx(
+                    out=bank[:, t, :], lhsT=lhsT, lhsT_scale=lhsT_scale,
+                    rhs=v_w[a][:, cols].bitcast(FP8X4), rhs_scale=rhs_scale,
+                    start=((a, t) == steps[0]), stop=((a, t) == steps[-1]),
+                )
             return bank[:].rearrange("p t n -> p n t")
 
         early = tile([P, CHUNKS // 2, CHUNK, PACK], F32, "skill1_early", tag="w2_raw0")
@@ -187,7 +184,7 @@ def tile_list_kendo_panel_scores_kernel(
             spirit[c] = product(bank4, c, "w4")
             bank2 = psum.tile([P, 4, CHUNK], F32, name="bank_s2", tag="bank_s2", bufs=2)
             sums = product(bank2, c, "w2")
-            best[c] = ring.tile([P, CHUNK, PACK], F32, name="best", tag="pair", bufs=2)
+            best[c] = ring.tile([P, CHUNK, PACK], F32, name="best", tag="pair", bufs=3)
             nc.vector.tensor_tensor(out=best[c][:], in0=sums, in1=skill1[c], op=ALU.max)
 
         def cap(c):
@@ -205,12 +202,12 @@ def tile_list_kendo_panel_scores_kernel(
             rows = slice(m * P, (m + 1) * P)
             bank = psum.tile([P, HALF], F32, name="bank_a", tag="bank_a", bufs=3)
             nc.tensor.matmul_mx(
-                out=bank[:], lhsT=v2_w[:, rows].bitcast(FP8X4), lhsT_scale=v2_s[:, rows],
+                out=bank[:], lhsT=v2_w[:, rows].bitcast(FP8X4), lhsT_scale=v2_s[8:P, rows],
                 rhs=h_c[u][:].bitcast(FP8X4), rhs_scale=h_s[u][:], start=True, stop=True,
             )
             bent = ring.tile([P, HALF], F32, name="bent", tag="bent", bufs=2)
             nc.scalar.activation(out=bent[:], in_=bank[:], func=ACT.Tanh)
-            scores[(m, u)] = ring.tile([P, HALF], F32, name="scores", tag="pair", bufs=2)
+            scores[(m, u)] = ring.tile([P, HALF], F32, name="scores", tag="pair", bufs=3)
             nc.scalar.activation(
                 out=scores[(m, u)][:], in_=bent[:], func=ACT.Identity,
                 scale=gain[:, m : m + 1], bias=shift[:, m : m + 1],

@@ -76,14 +76,15 @@ def tile_list_kendo_panel_scores_kernel(
             nc.sync.dma_start(
                 out=tab_s[32 * q : 32 * q + 8, :].bitcast(I32), in_=tab_scales[:, 4 * q : 4 * q + 4, :].bitcast(I32)
             )
-        load_words(tab_w[0], tab_words[0])
         w1_raw0 = load_weight(w1, 0, whole, "w1_raw0")
+        load_words(tab_w[0], tab_words[0])
         load_scale_rows(w4s_raw, w4_scales)
         w1_raw1 = load_weight(w1, 1, whole, "w1_raw1")
         nc.sync.dma_start(idx2[:], offs2)
         load_scale_rows(tab2_s[:].rearrange("p (a n) -> p a n", a=1), tab2_scales, first=8)
         load_words(tab_w[1], tab_words[1])
-        w2_raw0 = load_weight(w2, 0, whole, "w2_raw0")
+        w2_raw0l = load_weight(w2, 0, low, "w2_raw0l")
+        w2_raw0h = load_weight(w2, 0, high, "w2_raw0h")
         w2_raw1l = load_weight(w2, 1, low, "w2_raw1l")
         w2_raw1h = load_weight(w2, 1, high, "w2_raw1h")
         load_words(tab2_w, tab2_words[0])
@@ -132,7 +133,8 @@ def tile_list_kendo_panel_scores_kernel(
         gather(v_w[0], tab_w[0][:], idx, 0, S)
         round_weight(nc.scalar.copy, ("w1", 0), w1_raw0, whole)
         round_weight(nc.scalar.copy, ("w1", 1), w1_raw1, whole)
-        round_weight(nc.scalar.copy, ("w2", 0), w2_raw0, whole)
+        round_weight(nc.scalar.copy, ("w2", 0), w2_raw0l, low)
+        round_weight(nc.scalar.copy, ("w2", 0), w2_raw0h, high)
         w4_s = tile([P, PASSES, H], U8, "w4_s")
         nc.vector.tensor_copy(
             out=w4_s[:].rearrange("p a (t m) -> p a t m", t=4), in_=w4s_raw[:].rearrange("p a (m t) -> p a t m", t=4)
@@ -165,7 +167,7 @@ def tile_list_kendo_panel_scores_kernel(
                 )
             return bank[:].rearrange("p t n -> p n t")
 
-        early = tile([P, CHUNKS // 2, CHUNK, PACK], F32, "skill1_early", tag="w2_raw0")
+        early = tile([P, CHUNKS // 2, CHUNK, PACK], F32, "skill1_early", tag="w2_raw0h")
         late = tile([P, CHUNKS // 2, CHUNK, PACK], F32, "skill1_late")
         skill1 = [part[:, c] for part in (early, late) for c in range(CHUNKS // 2)]
         best = {}

from contextlib import ExitStack

import concourse.mybir as mybir

K, T, S, H, T3, S2, T2 = 1024, 2048, 1024, 512, 2048, 512, 2048
FLOPS = 2 * (3 * K * H * S + H * S2 * S)

F32 = mybir.dt.float32
BF16 = mybir.dt.bfloat16
I32 = mybir.dt.int32
U32 = mybir.dt.uint32
U16 = mybir.dt.uint16
U8 = mybir.dt.uint8
FP8X4 = mybir.dt.float8_e4m3fn_x4
FP4X4 = mybir.dt.float4_e2m1fn_x4
ACT = mybir.ActivationFunctionType
ALU = mybir.AluOpType

P = 128
PACK = 4
PASSES = K // (P * PACK)
CHUNK = 128
CHUNKS = S // CHUNK
HALF = 512
M_TILES = S2 // P


def tile_list_kendo_panel_scores_kernel(
    tc, tab_words, tab_scales, offs, w1, w2, w4_words, w4_scales, tab2_words, tab2_scales, offs2,
    grade_gain, grade_shift, offs3, wgo, page1, out,
):
    nc = tc.nc
    with ExitStack() as ctx:
        keep = ctx.enter_context(tc.tile_pool(name="keep", bufs=1))
        ring = ctx.enter_context(tc.tile_pool(name="ring", bufs=2))
        psum = ctx.enter_context(tc.psum_pool(name="psum", bufs=1))

        def tile(shape, dtype, name, tag=None):
            return keep.tile(shape, dtype, name=name, tag=tag or name, align_bytes=64)

        idx = tile([P, S // 16], U16, "idx")
        idx2 = tile([P, S2 // 16], U16, "idx2")
        idx3 = tile([P, S // 16], U16, "idx3")

        tab_w = [tile([P, T], U32, "tab_w%d" % a) for a in range(PASSES)]
        tab_s = tile([P, T], U8, "tab_s")
        tab2_w = tile([P, T3], U32, "tab2_w")
        tab2_s = tile([P, T3], U8, "tab2_s")
        w4_raw = tile([P, PASSES, H], U16, "w4_raw")
        w4s_raw = tile([P, PASSES, H], U8, "w4s_raw")

        nc.vector.memset(tab_s[:].bitcast(I32), 0)
        nc.vector.memset(w4s_raw[:].bitcast(I32), 0)
        nc.vector.memset(tab2_s[:].bitcast(I32), 0)
        v_s_low = tile([P, S], U8, "v_s_low")
        nc.vector.memset(v_s_low[:].bitcast(I32), 0)

        def load_scale_rows(dst, src, first=0):
            rows = src.rearrange("a (q r) n -> r q a n", r=4)
            for r in range(4):
                nc.sync.dma_start(out=dst[first + r : P : 32].bitcast(I32), in_=rows[r].bitcast(I32))

        def load_words(dst, src):
            nc.sync.dma_start(out=dst[:].bitcast(I32), in_=src.rearrange("p t i -> p (t i)").bitcast(I32))

        def load_weight(w, a, cols, name):
            raw = tile([P, PACK, cols.stop - cols.start], F32, name)
            rows = w[a * 512 : (a + 1) * 512, cols].rearrange("(p j) c -> p j c", j=PACK)
            nc.sync.dma_start(out=raw[:], in_=rows)
            return raw

        whole, low, high = slice(0, H), slice(0, H // 2), slice(H // 2, H)
        nc.sync.dma_start(idx[:], offs)
        nc.sync.dma_start(out=w4_raw[:].bitcast(I32), in_=w4_words.rearrange("a p n -> p a n").bitcast(I32))
        for q in range(4):
            nc.sync.dma_start(
                out=tab_s[32 * q : 32 * q + 8, :].bitcast(I32), in_=tab_scales[:, 4 * q : 4 * q + 4, :].bitcast(I32)
            )
        w1_raw0 = load_weight(w1, 0, whole, "w1_raw0")
        load_words(tab_w[0], tab_words[0])
        load_scale_rows(w4s_raw, w4_scales)
        w1_raw1 = load_weight(w1, 1, whole, "w1_raw1")
        nc.sync.dma_start(idx2[:], offs2)
        load_scale_rows(tab2_s[:].rearrange("p (a n) -> p a n", a=1), tab2_scales, first=8)
        load_words(tab_w[1], tab_words[1])
        w2_raw0l = load_weight(w2, 0, low, "w2_raw0l")
        w2_raw0h = load_weight(w2, 0, high, "w2_raw0h")
        w2_raw1l = load_weight(w2, 1, low, "w2_raw1l")
        w2_raw1h = load_weight(w2, 1, high, "w2_raw1h")
        load_words(tab2_w, tab2_words[0])
        nc.sync.dma_start(idx3[:], offs3)
        gain = tile([P, M_TILES], F32, "gain")
        shift = tile([P, M_TILES], F32, "shift")
        with nc.allow_non_contiguous_dma(reason="one value a partition"):
            nc.sync.dma_start(out=gain[:], in_=grade_gain.rearrange("(c p) -> p c", p=P))
            nc.sync.dma_start(out=shift[:], in_=grade_shift.rearrange("(c p) -> p c", p=P))
        wgo_sb = tile([P, S], F32, "wgo_sb")
        nc.sync.dma_start(out=wgo_sb[:], in_=wgo)
        pages = [tile([P, T2], F32, "page%d" % m) for m in range(M_TILES)]
        for m in range(M_TILES):
            nc.sync.dma_start(out=pages[m][:], in_=page1[m * P : (m + 1) * P, :])

        v_w = [tile([P, S], U32, "v_w%d" % a) for a in range(PASSES)]
        v_s = tile([P, S], U8, "v_s")
        v2_w = tile([P, S2], U32, "v2_w")
        v2_s = tile([P, S2], U8, "v2_s")

        def gather(dst, window, offsets, j0, j1):
            nc.vector.tensor_copy(dst[:, j0:j1], window.indirect(offsets[:, j0 // 16 : j1 // 16]))

        rounded = {}
        codes = {}
        planes = {}

        def round_weight(copy, key, raw, cols):
            if key not in rounded:
                rounded[key] = tile([P, PACK * H], BF16, "rounded_%s%d" % key)
            m_range = slice(cols.start // 4, cols.stop // 4)
            dst = rounded[key][:].rearrange("p (t m j) -> p m j t", t=4, j=PACK)[:, m_range]
            copy(out=dst, in_=raw[:].rearrange("p j (m t) -> p m j t", t=4))

        def quantize_weight(key):
            codes[key] = tile([P, H], U32, "codes_%s%d" % key)
            planes[key] = tile([P, H], U8, "plane_%s%d" % key)
            nc.vector.quantize_mx(out=codes[key][:].bitcast(FP8X4), scales=planes[key][:], in_=rounded[key][:])

        w4_c = tile([P, PASSES, H], U16, "w4_c")
        nc.vector.tensor_copy(
            out=w4_c[:].rearrange("p a (t m) -> p a t m", t=4), in_=w4_raw[:].rearrange("p a (m t) -> p a t m", t=4)
        )
        gather(v_s, tab_s[:], idx, 0, S)
        nc.gpsimd.dma_start(out=v_s_low[0:100, :].bitcast(I32), in_=v_s[4:104, :].bitcast(I32))
        gather(v_w[0], tab_w[0][:], idx, 0, S)
        round_weight(nc.scalar.copy, ("w1", 0), w1_raw0, whole)
        round_weight(nc.scalar.copy, ("w1", 1), w1_raw1, whole)
        round_weight(nc.scalar.copy, ("w2", 0), w2_raw0l, low)
        round_weight(nc.scalar.copy, ("w2", 0), w2_raw0h, high)
        w4_s = tile([P, PASSES, H], U8, "w4_s")
        nc.vector.tensor_copy(
            out=w4_s[:].rearrange("p a (t m) -> p a t m", t=4), in_=w4s_raw[:].rearrange("p a (m t) -> p a t m", t=4)
        )
        quantize_weight(("w1", 0))
        gather(v2_s, tab2_s[:], idx2, 0, S2)
        quantize_weight(("w1", 1))
        gather(v_w[1], tab_w[1][:], idx, 0, 256)
        gather(v_w[1], tab_w[1][:], idx, 256, S)
        round_weight(nc.vector.tensor_copy, ("w2", 1), w2_raw1l, low)
        quantize_weight(("w2", 0))
        round_weight(nc.vector.tensor_copy, ("w2", 1), w2_raw1h, high)
        quantize_weight(("w2", 1))

        def product(bank, c, weight):
            cols = slice(c * CHUNK, (c + 1) * CHUNK)
            steps = [(a, t) for a in range(PASSES) for t in range(4)]
            for a, t in steps:
                stat = slice(t * P, (t + 1) * P)
                if weight == "w4":
                    lhsT, lhsT_scale = w4_c[:, a, stat].bitcast(FP4X4), w4_s[:, a, stat]
                    rhs_scale = (v_s, v_s_low)[a][:, cols]
                else:
                    lhsT, lhsT_scale = codes[(weight, a)][:, stat].bitcast(FP8X4), planes[(weight, a)][:, stat]
                    rhs_scale = v_s[4 * a : P, cols]
                nc.tensor.matmul_mx(
                    out=bank[:, t, :], lhsT=lhsT, lhsT_scale=lhsT_scale,
                    rhs=v_w[a][:, cols].bitcast(FP8X4), rhs_scale=rhs_scale,
                    start=((a, t) == steps[0]), stop=((a, t) == steps[-1]),
                )
            return bank[:].rearrange("p t n -> p n t")

        early = tile([P, CHUNKS // 2, CHUNK, PACK], F32, "skill1_early", tag="w2_raw0h")
        late = tile([P, CHUNKS // 2, CHUNK, PACK], F32, "skill1_late")
        skill1 = [part[:, c] for part in (early, late) for c in range(CHUNKS // 2)]
        best = {}
        spirit = {}
        h_bf = [tile([P, HALF, PACK], BF16, "h_bf%d" % u) for u in range(2)]
        h_c = [tile([P, HALF], U32, "h_c%d" % u) for u in range(2)]
        h_s = [tile([P, HALF], U8, "h_s%d" % u) for u in range(2)]

        def first_reading(c):
            bank = psum.tile([P, 4, CHUNK], F32, name="bank_a", tag="bank_a", bufs=3)
            sums = product(bank, c, "w1")
            nc.scalar.copy(out=skill1[c], in_=sums)

        def better_reading(c):
            bank4 = psum.tile([P, 4, CHUNK], F32, name="bank_sp", tag="bank_sp", bufs=3)
            spirit[c] = product(bank4, c, "w4")
            bank2 = psum.tile([P, 4, CHUNK], F32, name="bank_s2", tag="bank_s2", bufs=2)
            sums = product(bank2, c, "w2")
            best[c] = ring.tile([P, CHUNK, PACK], F32, name="best", tag="pair", bufs=3)
            nc.vector.tensor_tensor(out=best[c][:], in0=sums, in1=skill1[c], op=ALU.max)

        def cap(c):
            u, n0 = divmod(c * CHUNK, HALF)
            nc.vector.tensor_tensor(out=h_bf[u][:, n0 : n0 + CHUNK, :], in0=spirit[c], in1=best[c][:], op=ALU.min)

        def quantize_h(u):
            nc.vector.quantize_mx(
                out=h_c[u][:].bitcast(FP8X4), scales=h_s[u][:], in_=h_bf[u][:].rearrange("p n t -> p (n t)")
            )

        scores = {}

        def score(m, u):
            rows = slice(m * P, (m + 1) * P)
            bank = psum.tile([P, HALF], F32, name="bank_a", tag="bank_a", bufs=3)
            nc.tensor.matmul_mx(
                out=bank[:], lhsT=v2_w[:, rows].bitcast(FP8X4), lhsT_scale=v2_s[8:P, rows],
                rhs=h_c[u][:].bitcast(FP8X4), rhs_scale=h_s[u][:], start=True, stop=True,
            )
            bent = ring.tile([P, HALF], F32, name="bent", tag="bent", bufs=2)
            nc.scalar.activation(out=bent[:], in_=bank[:], func=ACT.Tanh)
            scores[(m, u)] = ring.tile([P, HALF], F32, name="scores", tag="pair", bufs=3)
            nc.scalar.activation(
                out=scores[(m, u)][:], in_=bent[:], func=ACT.Identity,
                scale=gain[:, m : m + 1], bias=shift[:, m : m + 1],
            )

        def put(m, u):
            j0, j1 = u * HALF, (u + 1) * HALF
            nc.vector.tensor_tensor(
                out=pages[m][:].indirect(idx3[:, j0 // 16 : j1 // 16]),
                in0=scores[(m, u)][:], in1=wgo_sb[:, j0:j1], op=ALU.mult,
            )

        def store(m):
            nc.sync.dma_start(out=out[m * P : (m + 1) * P, :], in_=pages[m][:])

        def finish(m, u):
            score(m, u)
            put(m, u)
            if u == 1:
                store(m)

        ahead = 3
        for c in range(ahead):
            first_reading(c)
        for c in range(CHUNKS):
            better_reading(c)
            if c + ahead < CHUNKS:
                first_reading(c + ahead)
            if c > 0:
                cap(c - 1)
            if c == 2:
                gather(v2_w, tab2_w[:], idx2, 0, S2)
            if c == CHUNKS // 2:
                quantize_h(0)
            if c in (5, 6):
                finish(c - 5, 0)
        cap(CHUNKS - 1)
        quantize_h(1)
        for m in range(2, M_TILES):
            finish(m, 0)
        for m in range(M_TILES):
            finish(m, 1)
